import numpy as np
import ml_dtypes


def mxq(x, axis, fmt="e4m3"):
    dtype, down = {"e4m3": (ml_dtypes.float8_e4m3fn, 7), "e5m2": (ml_dtypes.float8_e5m2, 14)}[fmt]
    v = np.moveaxis(np.asarray(x, np.float32).astype(ml_dtypes.bfloat16).astype(np.float64), axis, -1)
    blocks = v.reshape(v.shape[:-1] + (-1, 32))
    amax = np.abs(blocks).max(-1, keepdims=True)
    byte = np.maximum(np.where(amax > 0, np.frexp(amax)[1] - 1 + 127, 0) - down, 1)
    scale = np.exp2(byte - 127.0)
    codes = (blocks / scale).astype(np.float32).astype(dtype).astype(np.float64)
    return np.moveaxis((codes * scale).reshape(v.shape), -1, axis)


WIDE = False


def mx_kscale(k):
    if not WIDE:
        return np.ones(k)
    levels = np.array([10, -10, 5, -5, 0])
    if k % 512:
        return np.exp2(np.random.permutation(np.resize(levels, k // 32))).repeat(32)
    a = np.empty((k // 512, 16))
    for p in range(k // 512):
        a[p, :8] = np.random.permutation(np.resize(levels, 8))
        for g in range(8):
            far = levels[np.abs(levels - a[p, g]) >= 10]
            a[p, g + 8] = far[np.random.randint(len(far))]
    return np.exp2(a.ravel()).repeat(32)


def f64(x):
    return np.asarray(x).astype(np.float64)


def striped(idx):
    return np.tile(np.asarray(idx).reshape(-1, 16).T, (8, 1)).astype(np.uint16)


def unstriped(offs):
    return offs[:16].T.reshape(-1).astype(np.int64)


E2M1 = np.array([0.0, 0.5, 1.0, 1.5, 2.0, 3.0, 4.0, 6.0, -0.0, -0.5, -1.0, -1.5, -2.0, -3.0, -4.0, -6.0])


def pack_weight(w, fmt):
    k, n = w.shape
    w = f64(np.asarray(w, np.float32).astype(ml_dtypes.bfloat16)).reshape(k // 32, 32, n)
    amax = np.abs(w).max(1)
    if fmt == "e4m3":
        byte = np.frexp(amax)[1] - 1 + 127 - 7
    else:
        mant, ex = np.frexp(amax / 6.0)
        byte = np.where(mant > 0.5, ex, ex - 1) + 127
    byte = np.clip(np.where(amax > 0, byte, 1), 1, 254)
    scaled = (w * np.exp2(127.0 - byte)[:, None, :]).reshape(k, n).astype(np.float32)
    by_word = np.ascontiguousarray(scaled.reshape(k // 512, 128, 4, n).transpose(0, 1, 3, 2))
    if fmt == "e4m3":
        words = by_word.astype(ml_dtypes.float8_e4m3fn).view(np.uint8)
    else:
        c = by_word.astype(ml_dtypes.float4_e2m1fn).view(np.uint8) & 0xF
        words = (c[..., 0::2] | (c[..., 1::2] << 4)).reshape(k // 512, 128, 2 * n)
    return np.ascontiguousarray(words), np.ascontiguousarray(byte.astype(np.uint8).reshape(k // 512, 16, n))


def unpack_weight(words, scales, fmt):
    g, _, n = scales.shape
    words = np.ascontiguousarray(words).reshape(g, 128, n, -1)
    if fmt == "e4m3":
        vals = words.view(ml_dtypes.float8_e4m3fn).astype(np.float64)
    else:
        nib = np.empty((g, 128, n, 4), np.uint8)
        nib[..., 0::2] = words & 0xF
        nib[..., 1::2] = words >> 4
        vals = E2M1[nib]
    vals = vals * np.repeat(np.exp2(scales.astype(np.float64) - 127.0), 8, axis=1)[..., None]
    return vals.transpose(0, 1, 3, 2).reshape(g * 512, n)


D, K, U, I, E = 512, 512, 1024, 512, 256


def setup_inputs():
    n = np.random.standard_normal
    idx = np.random.permutation(U)[:I]
    idx2 = np.random.permutation(U)[:I]
    idx3 = np.random.permutation(U)[:I]
    fd = mx_kscale(D)
    fk = mx_kscale(K)
    notesp = pack_weight(n((D, U)) / fd[:, None], "e4m3")
    wbp = pack_weight(n((D, K)) * 1.0 / np.sqrt(D) * fd[:, None], "e2m1")
    wop = pack_weight(n((K, E)) * 1.0 / np.sqrt(K) / fk[:, None], "e4m3")
    return {
        "notes_words": notesp[0],
        "notes_scales": notesp[1],
        "wb_words": wbp[0],
        "wb_scales": wbp[1],
        "lam": (np.random.uniform(0.5, 1.5, (K, 1))).astype(np.float32),
        "kf": (np.random.uniform(0.5, 2.0, (K, 1)) * fk[:, None]).astype(np.float32),
        "wo_words": wop[0],
        "wo_scales": wop[1],
        "offs": striped(idx),
        "offs2": striped(idx2),
        "offs3": striped(idx3),
    }


def reference(notes_words, notes_scales, wb_words, wb_scales, lam, kf, wo_words, wo_scales, offs, offs2, offs3):
    idx = unstriped(offs)
    idx2 = unstriped(offs2)
    idx3 = unstriped(offs3)
    notesu = unpack_weight(notes_words, notes_scales, "e4m3")
    wbu = unpack_weight(wb_words, wb_scales, "e2m1")
    wou = unpack_weight(wo_words, wo_scales, "e4m3")
    h1 = wbu.T @ notesu
    f1 = np.zeros((K, U))
    f1[:, idx2] = h1[:, idx]
    c1 = h1 + f1 * f64(lam)
    v = c1[:, idx3] - h1[:, idx]
    w = v * f64(kf)
    wq = mxq(w, 0, "e4m3")
    y = wou.T @ wq
    return y

@@ -1,0 +1,195 @@
+from contextlib import ExitStack
+
+import concourse.mybir as mybir
+
+D, K, U, I, E = 512, 512, 1024, 512, 256
+FLOPS = 2 * D * K * U + 2 * K * E * I
+
+F32 = mybir.dt.float32
+BF16 = mybir.dt.bfloat16
+I32 = mybir.dt.int32
+U16 = mybir.dt.uint16
+U8 = mybir.dt.uint8
+FP8X4 = mybir.dt.float8_e4m3fn_x4
+FP4X4 = mybir.dt.float4_e2m1fn_x4
+COPY = mybir.ActivationFunctionType.Copy
+MULT = mybir.AluOpType.mult
+ADD = mybir.AluOpType.add
+SUB = mybir.AluOpType.subtract
+
+P = 128
+PACK = 4
+BANK = 512
+HALF = I // 2
+
+
+def load_scales(nc, plane, scales):
+    for q in range(4):
+        nc.sync.dma_start(out=plane.bitcast(I32)[32 * q : 32 * q + 4, :], in_=scales[0, 4 * q : 4 * q + 4, :].bitcast(I32))
+
+
+def tile_attend_hiddenhop_kernel(tc, notes_words, notes_scales, wb_words, wb_scales, lam, kf, wo_words, wo_scales, offs, offs2, offs3, out):
+    nc = tc.nc
+    with ExitStack() as ctx:
+        keep = ctx.enter_context(tc.tile_pool(name="keep", bufs=1))
+        psum = ctx.enter_context(tc.psum_pool(name="psum", bufs=1))
+
+        picks = keep.tile([P, I // 16], U16, name="picks")
+        places = keep.tile([P, I // 16], U16, name="places")
+        reads = keep.tile([P, I // 16], U16, name="reads")
+        wb_raw = keep.tile([P, 2 * K], U8, name="wb_raw", align_bytes=64)
+        wb_raw_sc = keep.tile([P, K], U8, name="wb_raw_sc", align_bytes=64)
+        wb_codes = keep.tile([P, 2 * K], U8, name="wb_codes", align_bytes=64)
+        wb_sc = keep.tile([P, K], U8, name="wb_sc", align_bytes=64)
+        notes = [keep.tile([P, 4 * BANK], U8, name=f"notes{b}", align_bytes=64) for b in range(2)]
+        notes_sc = keep.tile([P, U], U8, name="notes_sc", align_bytes=64)
+        h1 = [keep.tile([P, U], F32, name=f"h1_{t}", align_bytes=64) for t in range(PACK)]
+        windows = [keep.tile([P, U], F32, name=f"f1_{j}") for j in range(3)]
+        f1 = [windows[0], windows[1], windows[2], windows[1]]
+        sums = [keep.tile([P, U], F32, name=f"c1_{j}") for j in range(2)]
+        c1 = [sums[1], sums[0], sums[0], sums[0]]
+        picked = [keep.tile([P, I], F32, name=f"picked{t}") for t in range(PACK)]
+        v = [keep.tile([P, I], F32, name=f"v{t}") for t in range(PACK - 1)]
+        w_codes = keep.tile([P, 4 * I], U8, name="w_codes", align_bytes=64)
+        w_sc = keep.tile([P, I], U8, name="w_sc", align_bytes=64)
+
+        nc.vector.memset(wb_raw_sc[:].bitcast(I32), 0)
+        nc.vector.memset(notes_sc[:].bitcast(I32), 0)
+        notes_rows = notes_words[0].rearrange("p u r -> p (u r)")
+        nc.sync.dma_start(picks[:], offs)
+        nc.sync.dma_start(out=wb_raw[:].bitcast(I32), in_=wb_words[0].bitcast(I32))
+        nc.sync.dma_start(out=notes[0][:].bitcast(I32), in_=notes_rows[:, 0 : 4 * BANK].bitcast(I32))
+        load_scales(nc, wb_raw_sc[:], wb_scales)
+        nc.sync.dma_start(out=notes[1][:].bitcast(I32), in_=notes_rows[:, 4 * BANK : 8 * BANK].bitcast(I32))
+        load_scales(nc, notes_sc[:], notes_scales)
+        nc.sync.dma_start(places[:], offs2)
+        nc.sync.dma_start(reads[:], offs3)
+        for window in windows:
+            nc.vector.memset(window[:], 0.0)
+
+        nc.vector.tensor_copy(
+            out=wb_codes[:].bitcast(U16).rearrange("p (t m) -> p m t", t=PACK),
+            in_=wb_raw[:].bitcast(U16).rearrange("p (m t) -> p m t", t=PACK),
+        )
+        nc.vector.tensor_copy(
+            out=wb_sc[:].rearrange("p (t m) -> p m t", t=PACK),
+            in_=wb_raw_sc[:].rearrange("p (m t) -> p m t", t=PACK),
+        )
+
+        lam_t = keep.tile([P, PACK], F32, name="lam_t", tag="wb_raw", align_bytes=64)
+        nc.sync.dma_start(out=lam_t[:], in_=lam.rearrange("(p t) o -> p (t o)", t=PACK))
+        wo_sc = wb_raw_sc[:, 0:E]
+        load_scales(nc, wo_sc, wo_scales)
+
+        def multiply(t, b):
+            bank = psum.tile([P, BANK], F32, name=f"h1_bank{t}{b}", tag=f"bank{2 * t + b}")
+            nc.tensor.matmul_mx(
+                out=bank[:],
+                lhsT=wb_codes[:, 2 * P * t : 2 * P * (t + 1)].bitcast(FP4X4),
+                lhsT_scale=wb_sc[:, P * t : P * (t + 1)],
+                rhs=notes[b][:].bitcast(FP8X4),
+                rhs_scale=notes_sc[:, BANK * b : BANK * (b + 1)],
+                start=True,
+                stop=True,
+            )
+            return bank
+
+        def empty_on_scalar(t, b):
+            nc.scalar.copy(out=h1[t][:, BANK * b : BANK * (b + 1)], in_=multiply(t, b)[:])
+
+        def empty_on_vector(t, b):
+            nc.vector.tensor_copy(out=h1[t][:, BANK * b : BANK * (b + 1)], in_=multiply(t, b)[:])
+
+        def pick_on_vector(t):
+            nc.vector.tensor_copy(out=picked[t][:], in_=h1[t][:].indirect(picks[:]))
+
+        def pick_on_scalar(t):
+            nc.scalar.activation(out=picked[t][:], in_=h1[t][:].indirect(picks[:]), func=COPY)
+
+        def place_on_scalar(t):
+            for h in range(2):
+                nc.scalar.activation(
+                    out=f1[t][:].indirect(places[:, 16 * h : 16 * (h + 1)]),
+                    in_=picked[t][:, HALF * h : HALF * (h + 1)],
+                    func=COPY,
+                )
+
+        def combine(t):
+            nc.vector.scalar_tensor_tensor(out=c1[t][:], in0=f1[t][:], scalar=lam_t[:, t : t + 1], in1=h1[t][:], op0=MULT, op1=ADD)
+
+        def differ(t):
+            nc.vector.tensor_tensor(out=v[t][:], in0=c1[t][:].indirect(reads[:]), in1=picked[t][:], op=SUB)
+
+        empty_on_scalar(0, 0)
+        empty_on_vector(0, 1)
+        pick_on_scalar(0)
+        place_on_scalar(0)
+        empty_on_vector(1, 0)
+        empty_on_vector(1, 1)
+        pick_on_vector(1)
+        nc.vector.tensor_copy(out=f1[1][:].indirect(places[:]), in_=picked[1][:])
+        empty_on_scalar(2, 0)
+        empty_on_scalar(2, 1)
+        pick_on_scalar(2)
+        empty_on_scalar(3, 0)
+        empty_on_vector(3, 1)
+        wo_codes = keep.tile([P, 4 * E], U8, name="wo_codes", tag="notes0", align_bytes=64)
+        nc.sync.dma_start(out=wo_codes[:].bitcast(I32), in_=wo_words[0].rearrange("p e r -> p (e r)").bitcast(I32))
+        kf_t = keep.tile([P, PACK], F32, name="kf_t", tag="notes1", align_bytes=64)
+        nc.sync.dma_start(out=kf_t[:], in_=kf.rearrange("(p t) o -> p (t o)", t=PACK))
+        pick_on_vector(3)
+        place_on_scalar(2)
+        combine(1)
+        combine(0)
+        differ(1)
+        place_on_scalar(3)
+        differ(0)
+        combine(2)
+        differ(2)
+        last = PACK - 1
+        combine(last)
+        halves = [slice(HALF * h, HALF * (h + 1)) for h in range(2)]
+        v_last = [keep.tile([P, HALF], F32, name=f"v_last{h}") for h in range(2)]
+        for h in range(2):
+            nc.vector.tensor_tensor(
+                out=v_last[h][:], in0=c1[last][:].indirect(reads[:, 16 * h : 16 * (h + 1)]), in1=picked[last][:, halves[h]], op=SUB
+            )
+        w_planes = [
+            keep.tile([P, PACK, HALF], BF16, name="w_planes0", tag="h1_2", align_bytes=64),
+            keep.tile([P, PACK, HALF], BF16, name="w_planes1", tag="picked2"),
+        ]
+        for h in range(2):
+            for t in range(last):
+                nc.scalar.activation(out=w_planes[h][:, t, :], in_=v[t][:, halves[h]], func=COPY, scale=kf_t[:, t : t + 1])
+        nc.scalar.activation(out=w_planes[0][:, last, :], in_=v_last[0][:], func=COPY, scale=kf_t[:, last : last + 1])
+        nc.vector.tensor_scalar(out=w_planes[1][:, last, :], in0=v_last[1][:], scalar1=kf_t[:, last : last + 1], scalar2=None, op0=MULT)
+        w_woven = [keep.tile([P, HALF, PACK], BF16, name=f"w_woven{h}", align_bytes=64) for h in range(2)]
+        for h, copy in ((0, nc.scalar.copy), (1, nc.vector.tensor_copy)):
+            copy(
+                out=w_woven[h][:].rearrange("p (c i) t -> p c t i", i=4),
+                in_=w_planes[h][:].rearrange("p t (c i) -> p c t i", i=4),
+            )
+        for h in (1, 0):
+            nc.vector.quantize_mx(
+                out=w_codes[:, 4 * HALF * h : 4 * HALF * (h + 1)].bitcast(FP8X4),
+                scales=w_sc[:, halves[h]],
+                in_=w_woven[h][:].rearrange("p i t -> p (i t)"),
+            )
+        for h in (1, 0):
+            for m in range(E // P):
+                acc = psum.tile([P, HALF], F32, name=f"acc{h}{m}", tag=f"bank{2 * h + m}")
+                nc.tensor.matmul_mx(
+                    out=acc[:],
+                    lhsT=wo_codes[:, 4 * P * m : 4 * P * (m + 1)].bitcast(FP8X4),
+                    lhsT_scale=wo_sc[:, P * m : P * (m + 1)],
+                    rhs=w_codes[:, 4 * HALF * h : 4 * HALF * (h + 1)].bitcast(FP8X4),
+                    rhs_scale=w_sc[:, HALF * h : HALF * (h + 1)],
+                    start=True,
+                    stop=True,
+                )
+                result = keep.tile([P, HALF], F32, name=f"result{h}{m}")
+                if h == 0 and m == 1:
+                    nc.vector.tensor_copy(out=result[:], in_=acc[:])
+                else:
+                    nc.scalar.copy(out=result[:], in_=acc[:])
+                nc.sync.dma_start(out=out[P * m : P * (m + 1), HALF * h : HALF * (h + 1)], in_=result[:])

@@ -19,13 +19,20 @@ SUB = mybir.AluOpType.subtract
 
 P = 128
 PACK = 4
+LAST = PACK - 1
 BANK = 512
+QUARTER = U // 4
 HALF = I // 2
+PER_COLUMN = 16
 
 
-def load_scales(nc, plane, scales):
+def entries(list_tile, first, stop):
+    return list_tile[:, first // PER_COLUMN : stop // PER_COLUMN]
+
+
+def load_scales(nc, tile, scales):
     for q in range(4):
-        nc.sync.dma_start(out=plane.bitcast(I32)[32 * q : 32 * q + 4, :], in_=scales[0, 4 * q : 4 * q + 4, :].bitcast(I32))
+        nc.sync.dma_start(out=tile.bitcast(I32)[32 * q : 32 * q + 4, :], in_=scales[0, 4 * q : 4 * q + 4, :].bitcast(I32))
 
 
 def tile_attend_hiddenhop_kernel(tc, notes_words, notes_scales, wb_words, wb_scales, lam, kf, wo_words, wo_scales, offs, offs2, offs3, out):
@@ -34,14 +41,14 @@ def tile_attend_hiddenhop_kernel(tc, notes_words, notes_scales, wb_words, wb_sca
         keep = ctx.enter_context(tc.tile_pool(name="keep", bufs=1))
         psum = ctx.enter_context(tc.psum_pool(name="psum", bufs=1))
 
-        picks = keep.tile([P, I // 16], U16, name="picks")
-        places = keep.tile([P, I // 16], U16, name="places")
-        reads = keep.tile([P, I // 16], U16, name="reads")
+        idx = keep.tile([P, I // PER_COLUMN], U16, name="idx")
+        idx2 = keep.tile([P, I // PER_COLUMN], U16, name="idx2")
+        idx3 = keep.tile([P, I // PER_COLUMN], U16, name="idx3")
         wb_raw = keep.tile([P, 2 * K], U8, name="wb_raw", align_bytes=64)
         wb_raw_sc = keep.tile([P, K], U8, name="wb_raw_sc", align_bytes=64)
         wb_codes = keep.tile([P, 2 * K], U8, name="wb_codes", align_bytes=64)
         wb_sc = keep.tile([P, K], U8, name="wb_sc", align_bytes=64)
-        notes = [keep.tile([P, 4 * BANK], U8, name=f"notes{b}", align_bytes=64) for b in range(2)]
+        notes = [keep.tile([P, 4 * BANK], U8, name=f"notes{b}", align_bytes=64) for b in range(U // BANK)]
         notes_sc = keep.tile([P, U], U8, name="notes_sc", align_bytes=64)
         h1 = [keep.tile([P, U], F32, name=f"h1_{t}", align_bytes=64) for t in range(PACK)]
         windows = [keep.tile([P, U], F32, name=f"f1_{j}") for j in range(3)]
@@ -49,21 +56,21 @@ def tile_attend_hiddenhop_kernel(tc, notes_words, notes_scales, wb_words, wb_sca
         sums = [keep.tile([P, U], F32, name=f"c1_{j}") for j in range(2)]
         c1 = [sums[1], sums[0], sums[0], sums[0]]
         picked = [keep.tile([P, I], F32, name=f"picked{t}") for t in range(PACK)]
-        v = [keep.tile([P, I], F32, name=f"v{t}") for t in range(PACK - 1)]
+        v = [keep.tile([P, I], F32, name=f"v{t}") for t in range(LAST)]
         w_codes = keep.tile([P, 4 * I], U8, name="w_codes", align_bytes=64)
         w_sc = keep.tile([P, I], U8, name="w_sc", align_bytes=64)
 
         nc.vector.memset(wb_raw_sc[:].bitcast(I32), 0)
         nc.vector.memset(notes_sc[:].bitcast(I32), 0)
         notes_rows = notes_words[0].rearrange("p u r -> p (u r)")
-        nc.sync.dma_start(picks[:], offs)
+        nc.sync.dma_start(idx[:], offs)
         nc.sync.dma_start(out=wb_raw[:].bitcast(I32), in_=wb_words[0].bitcast(I32))
-        nc.sync.dma_start(out=notes[0][:].bitcast(I32), in_=notes_rows[:, 0 : 4 * BANK].bitcast(I32))
         load_scales(nc, wb_raw_sc[:], wb_scales)
-        nc.sync.dma_start(out=notes[1][:].bitcast(I32), in_=notes_rows[:, 4 * BANK : 8 * BANK].bitcast(I32))
+        for b in range(U // BANK):
+            nc.sync.dma_start(out=notes[b][:].bitcast(I32), in_=notes_rows[:, 4 * BANK * b : 4 * BANK * (b + 1)].bitcast(I32))
         load_scales(nc, notes_sc[:], notes_scales)
-        nc.sync.dma_start(places[:], offs2)
-        nc.sync.dma_start(reads[:], offs3)
+        nc.sync.dma_start(idx2[:], offs2)
+        nc.sync.dma_start(idx3[:], offs3)
         for window in windows:
             nc.vector.memset(window[:], 0.0)
 
@@ -81,115 +88,111 @@ def tile_attend_hiddenhop_kernel(tc, notes_words, notes_scales, wb_words, wb_sca
         wo_sc = wb_raw_sc[:, 0:E]
         load_scales(nc, wo_sc, wo_scales)
 
-        def multiply(t, b):
-            bank = psum.tile([P, BANK], F32, name=f"h1_bank{t}{b}", tag=f"bank{2 * t + b}")
+        def hidden(t, cols, bank, copy):
+            b, first = divmod(cols.start, BANK)
+            width = cols.stop - cols.start
+            acc = psum.tile([P, width], F32, name=f"h1_acc{t}_{cols.start}", tag=f"bank{bank}")
             nc.tensor.matmul_mx(
-                out=bank[:],
+                out=acc[:],
                 lhsT=wb_codes[:, 2 * P * t : 2 * P * (t + 1)].bitcast(FP4X4),
                 lhsT_scale=wb_sc[:, P * t : P * (t + 1)],
-                rhs=notes[b][:].bitcast(FP8X4),
-                rhs_scale=notes_sc[:, BANK * b : BANK * (b + 1)],
+                rhs=notes[b][:, 4 * first : 4 * (first + width)].bitcast(FP8X4),
+                rhs_scale=notes_sc[:, cols],
                 start=True,
                 stop=True,
             )
-            return bank
-
-        def empty_on_scalar(t, b):
-            nc.scalar.copy(out=h1[t][:, BANK * b : BANK * (b + 1)], in_=multiply(t, b)[:])
-
-        def empty_on_vector(t, b):
-            nc.vector.tensor_copy(out=h1[t][:, BANK * b : BANK * (b + 1)], in_=multiply(t, b)[:])
+            copy(out=h1[t][:, cols], in_=acc[:])
 
         def pick_on_vector(t):
-            nc.vector.tensor_copy(out=picked[t][:], in_=h1[t][:].indirect(picks[:]))
+            nc.vector.tensor_copy(out=picked[t][:], in_=h1[t][:].indirect(idx[:]))
 
         def pick_on_scalar(t):
-            nc.scalar.activation(out=picked[t][:], in_=h1[t][:].indirect(picks[:]), func=COPY)
+            nc.scalar.activation(out=picked[t][:], in_=h1[t][:].indirect(idx[:]), func=COPY)
+
+        def place_on_vector(t):
+            nc.vector.tensor_copy(out=f1[t][:].indirect(idx2[:]), in_=picked[t][:])
 
         def place_on_scalar(t):
-            for h in range(2):
+            for first in (0, HALF):
                 nc.scalar.activation(
-                    out=f1[t][:].indirect(places[:, 16 * h : 16 * (h + 1)]),
-                    in_=picked[t][:, HALF * h : HALF * (h + 1)],
-                    func=COPY,
+                    out=f1[t][:].indirect(entries(idx2, first, first + HALF)), in_=picked[t][:, first : first + HALF], func=COPY
                 )
 
         def combine(t):
             nc.vector.scalar_tensor_tensor(out=c1[t][:], in0=f1[t][:], scalar=lam_t[:, t : t + 1], in1=h1[t][:], op0=MULT, op1=ADD)
 
-        def differ(t):
-            nc.vector.tensor_tensor(out=v[t][:], in0=c1[t][:].indirect(reads[:]), in1=picked[t][:], op=SUB)
+        def differ(t, first, stop, into):
+            nc.vector.tensor_tensor(out=into, in0=c1[t][:].indirect(entries(idx3, first, stop)), in1=picked[t][:, first:stop], op=SUB)
 
-        empty_on_scalar(0, 0)
-        empty_on_vector(0, 1)
+        on_scalar, on_vector = nc.scalar.copy, nc.vector.tensor_copy
+        lower, upper = slice(0, BANK), slice(BANK, U)
+
+        for j in range(U // QUARTER):
+            hidden(0, slice(QUARTER * j, QUARTER * (j + 1)), j, (on_scalar, on_vector)[j % 2])
         pick_on_scalar(0)
         place_on_scalar(0)
-        empty_on_vector(1, 0)
-        empty_on_vector(1, 1)
+        hidden(1, lower, 4, on_vector)
+        hidden(1, upper, 5, on_vector)
         pick_on_vector(1)
-        nc.vector.tensor_copy(out=f1[1][:].indirect(places[:]), in_=picked[1][:])
-        empty_on_scalar(2, 0)
-        empty_on_scalar(2, 1)
+        place_on_vector(1)
+        hidden(2, lower, 6, on_scalar)
+        hidden(2, upper, 7, on_scalar)
         pick_on_scalar(2)
-        empty_on_scalar(3, 0)
-        empty_on_vector(3, 1)
+        hidden(3, lower, 0, on_scalar)
+        hidden(3, upper, 1, on_scalar)
         wo_codes = keep.tile([P, 4 * E], U8, name="wo_codes", tag="notes0", align_bytes=64)
         nc.sync.dma_start(out=wo_codes[:].bitcast(I32), in_=wo_words[0].rearrange("p e r -> p (e r)").bitcast(I32))
         kf_t = keep.tile([P, PACK], F32, name="kf_t", tag="notes1", align_bytes=64)
         nc.sync.dma_start(out=kf_t[:], in_=kf.rearrange("(p t) o -> p (t o)", t=PACK))
         pick_on_vector(3)
         place_on_scalar(2)
+
         combine(1)
         combine(0)
-        differ(1)
-        place_on_scalar(3)
-        differ(0)
+        differ(1, 0, I, v[1][:])
+        place_on_scalar(LAST)
+        differ(0, 0, I, v[0][:])
         combine(2)
-        differ(2)
-        last = PACK - 1
-        combine(last)
+        differ(2, 0, I, v[2][:])
+        combine(LAST)
+
         halves = [slice(HALF * h, HALF * (h + 1)) for h in range(2)]
         v_last = [keep.tile([P, HALF], F32, name=f"v_last{h}") for h in range(2)]
         for h in range(2):
-            nc.vector.tensor_tensor(
-                out=v_last[h][:], in0=c1[last][:].indirect(reads[:, 16 * h : 16 * (h + 1)]), in1=picked[last][:, halves[h]], op=SUB
+            differ(LAST, halves[h].start, halves[h].stop, v_last[h][:])
+        w_planes = keep.tile([P, 2, PACK, HALF], BF16, name="w_planes", tag="h1_2", align_bytes=64)
+        for t in range(LAST):
+            nc.scalar.activation(
+                out=w_planes[:, :, t, :], in_=v[t][:].rearrange("p (h i) -> p h i", h=2), func=COPY, scale=kf_t[:, t : t + 1]
             )
-        w_planes = [
-            keep.tile([P, PACK, HALF], BF16, name="w_planes0", tag="h1_2", align_bytes=64),
-            keep.tile([P, PACK, HALF], BF16, name="w_planes1", tag="picked2"),
-        ]
-        for h in range(2):
-            for t in range(last):
-                nc.scalar.activation(out=w_planes[h][:, t, :], in_=v[t][:, halves[h]], func=COPY, scale=kf_t[:, t : t + 1])
-        nc.scalar.activation(out=w_planes[0][:, last, :], in_=v_last[0][:], func=COPY, scale=kf_t[:, last : last + 1])
-        nc.vector.tensor_scalar(out=w_planes[1][:, last, :], in0=v_last[1][:], scalar1=kf_t[:, last : last + 1], scalar2=None, op0=MULT)
+        nc.scalar.activation(out=w_planes[:, 0, LAST, :], in_=v_last[0][:], func=COPY, scale=kf_t[:, LAST : LAST + 1])
+        nc.vector.tensor_scalar(out=w_planes[:, 1, LAST, :], in0=v_last[1][:], scalar1=kf_t[:, LAST : LAST + 1], scalar2=None, op0=MULT)
+
         w_woven = [keep.tile([P, HALF, PACK], BF16, name=f"w_woven{h}", align_bytes=64) for h in range(2)]
-        for h, copy in ((0, nc.scalar.copy), (1, nc.vector.tensor_copy)):
+        for h, copy in ((0, on_scalar), (1, on_vector)):
             copy(
                 out=w_woven[h][:].rearrange("p (c i) t -> p c t i", i=4),
-                in_=w_planes[h][:].rearrange("p t (c i) -> p c t i", i=4),
+                in_=w_planes[:, h, :, :].rearrange("p t (c i) -> p c t i", i=4),
             )
-        for h in (1, 0):
+        for h in range(2):
             nc.vector.quantize_mx(
                 out=w_codes[:, 4 * HALF * h : 4 * HALF * (h + 1)].bitcast(FP8X4),
                 scales=w_sc[:, halves[h]],
                 in_=w_woven[h][:].rearrange("p i t -> p (i t)"),
             )
-        for h in (1, 0):
+
+        for h in range(2):
             for m in range(E // P):
-                acc = psum.tile([P, HALF], F32, name=f"acc{h}{m}", tag=f"bank{2 * h + m}")
+                acc = psum.tile([P, HALF], F32, name=f"out_acc{h}{m}", tag=f"bank{2 + 2 * h + m}")
                 nc.tensor.matmul_mx(
                     out=acc[:],
                     lhsT=wo_codes[:, 4 * P * m : 4 * P * (m + 1)].bitcast(FP8X4),
                     lhsT_scale=wo_sc[:, P * m : P * (m + 1)],
                     rhs=w_codes[:, 4 * HALF * h : 4 * HALF * (h + 1)].bitcast(FP8X4),
-                    rhs_scale=w_sc[:, HALF * h : HALF * (h + 1)],
+                    rhs_scale=w_sc[:, halves[h]],
                     start=True,
                     stop=True,
                 )
                 result = keep.tile([P, HALF], F32, name=f"result{h}{m}")
-                if h == 0 and m == 1:
-                    nc.vector.tensor_copy(out=result[:], in_=acc[:])
-                else:
-                    nc.scalar.copy(out=result[:], in_=acc[:])
-                nc.sync.dma_start(out=out[P * m : P * (m + 1), HALF * h : HALF * (h + 1)], in_=result[:])
+                (on_scalar, on_vector)[m](out=result[:], in_=acc[:])
+                nc.sync.dma_start(out=out[P * m : P * (m + 1), halves[h]], in_=result[:])

from contextlib import ExitStack

import concourse.mybir as mybir

D, K, U, I, E = 512, 512, 1024, 512, 256
FLOPS = 2 * D * K * U + 2 * K * E * I

F32 = mybir.dt.float32
BF16 = mybir.dt.bfloat16
I32 = mybir.dt.int32
U16 = mybir.dt.uint16
U8 = mybir.dt.uint8
FP8X4 = mybir.dt.float8_e4m3fn_x4
FP4X4 = mybir.dt.float4_e2m1fn_x4
COPY = mybir.ActivationFunctionType.Copy
MULT = mybir.AluOpType.mult
ADD = mybir.AluOpType.add
SUB = mybir.AluOpType.subtract

P = 128
PACK = 4
LAST = PACK - 1
BANK = 512
QUARTER = U // 4
HALF = I // 2
PER_COLUMN = 16


def entries(list_tile, first, stop):
    return list_tile[:, first // PER_COLUMN : stop // PER_COLUMN]


def load_scales(nc, tile, scales):
    for q in range(4):
        nc.sync.dma_start(out=tile.bitcast(I32)[32 * q : 32 * q + 4, :], in_=scales[0, 4 * q : 4 * q + 4, :].bitcast(I32))


def tile_attend_hiddenhop_kernel(tc, notes_words, notes_scales, wb_words, wb_scales, lam, kf, wo_words, wo_scales, offs, offs2, offs3, out):
    nc = tc.nc
    with ExitStack() as ctx:
        keep = ctx.enter_context(tc.tile_pool(name="keep", bufs=1))
        psum = ctx.enter_context(tc.psum_pool(name="psum", bufs=1))

        idx = keep.tile([P, I // PER_COLUMN], U16, name="idx")
        idx2 = keep.tile([P, I // PER_COLUMN], U16, name="idx2")
        idx3 = keep.tile([P, I // PER_COLUMN], U16, name="idx3")
        wb_raw = keep.tile([P, 2 * K], U8, name="wb_raw", align_bytes=64)
        wb_raw_sc = keep.tile([P, K], U8, name="wb_raw_sc", align_bytes=64)
        wb_codes = keep.tile([P, 2 * K], U8, name="wb_codes", align_bytes=64)
        wb_sc = keep.tile([P, K], U8, name="wb_sc", align_bytes=64)
        notes = [keep.tile([P, 4 * BANK], U8, name=f"notes{b}", align_bytes=64) for b in range(U // BANK)]
        notes_sc = keep.tile([P, U], U8, name="notes_sc", align_bytes=64)
        h1 = [keep.tile([P, U], F32, name=f"h1_{t}", align_bytes=64) for t in range(PACK)]
        windows = [keep.tile([P, U], F32, name=f"f1_{j}") for j in range(3)]
        f1 = [windows[0], windows[1], windows[2], windows[1]]
        sums = [keep.tile([P, U], F32, name=f"c1_{j}") for j in range(2)]
        c1 = [sums[1], sums[0], sums[0], sums[0]]
        picked = [keep.tile([P, I], F32, name=f"picked{t}") for t in range(PACK)]
        v = [keep.tile([P, I], F32, name=f"v{t}") for t in range(LAST)]
        w_codes = keep.tile([P, 4 * I], U8, name="w_codes", align_bytes=64)
        w_sc = keep.tile([P, I], U8, name="w_sc", align_bytes=64)

        nc.vector.memset(wb_raw_sc[:].bitcast(I32), 0)
        nc.vector.memset(notes_sc[:].bitcast(I32), 0)
        notes_rows = notes_words[0].rearrange("p u r -> p (u r)")
        nc.sync.dma_start(idx[:], offs)
        nc.sync.dma_start(out=wb_raw[:].bitcast(I32), in_=wb_words[0].bitcast(I32))
        load_scales(nc, wb_raw_sc[:], wb_scales)
        for b in range(U // BANK):
            nc.sync.dma_start(out=notes[b][:].bitcast(I32), in_=notes_rows[:, 4 * BANK * b : 4 * BANK * (b + 1)].bitcast(I32))
        load_scales(nc, notes_sc[:], notes_scales)
        nc.sync.dma_start(idx2[:], offs2)
        nc.sync.dma_start(idx3[:], offs3)
        for window in windows:
            nc.vector.memset(window[:], 0.0)

        nc.vector.tensor_copy(
            out=wb_codes[:].bitcast(U16).rearrange("p (t m) -> p m t", t=PACK),
            in_=wb_raw[:].bitcast(U16).rearrange("p (m t) -> p m t", t=PACK),
        )
        nc.vector.tensor_copy(
            out=wb_sc[:].rearrange("p (t m) -> p m t", t=PACK),
            in_=wb_raw_sc[:].rearrange("p (m t) -> p m t", t=PACK),
        )

        lam_t = keep.tile([P, PACK], F32, name="lam_t", tag="wb_raw", align_bytes=64)
        nc.sync.dma_start(out=lam_t[:], in_=lam.rearrange("(p t) o -> p (t o)", t=PACK))
        wo_sc = wb_raw_sc[:, 0:E]
        load_scales(nc, wo_sc, wo_scales)

        def hidden(t, cols, bank, copy):
            b, first = divmod(cols.start, BANK)
            width = cols.stop - cols.start
            acc = psum.tile([P, width], F32, name=f"h1_acc{t}_{cols.start}", tag=f"bank{bank}")
            nc.tensor.matmul_mx(
                out=acc[:],
                lhsT=wb_codes[:, 2 * P * t : 2 * P * (t + 1)].bitcast(FP4X4),
                lhsT_scale=wb_sc[:, P * t : P * (t + 1)],
                rhs=notes[b][:, 4 * first : 4 * (first + width)].bitcast(FP8X4),
                rhs_scale=notes_sc[:, cols],
                start=True,
                stop=True,
            )
            copy(out=h1[t][:, cols], in_=acc[:])

        def pick_on_vector(t):
            nc.vector.tensor_copy(out=picked[t][:], in_=h1[t][:].indirect(idx[:]))

        def pick_on_scalar(t):
            nc.scalar.activation(out=picked[t][:], in_=h1[t][:].indirect(idx[:]), func=COPY)

        def place_on_vector(t):
            nc.vector.tensor_copy(out=f1[t][:].indirect(idx2[:]), in_=picked[t][:])

        def place_on_scalar(t):
            for first in (0, HALF):
                nc.scalar.activation(
                    out=f1[t][:].indirect(entries(idx2, first, first + HALF)), in_=picked[t][:, first : first + HALF], func=COPY
                )

        def combine(t):
            nc.vector.scalar_tensor_tensor(out=c1[t][:], in0=f1[t][:], scalar=lam_t[:, t : t + 1], in1=h1[t][:], op0=MULT, op1=ADD)

        def differ(t, first, stop, into):
            nc.vector.tensor_tensor(out=into, in0=c1[t][:].indirect(entries(idx3, first, stop)), in1=picked[t][:, first:stop], op=SUB)

        on_scalar, on_vector = nc.scalar.copy, nc.vector.tensor_copy
        lower, upper = slice(0, BANK), slice(BANK, U)

        for j in range(U // QUARTER):
            hidden(0, slice(QUARTER * j, QUARTER * (j + 1)), j, (on_scalar, on_vector)[j % 2])
        pick_on_scalar(0)
        place_on_scalar(0)
        hidden(1, lower, 4, on_vector)
        hidden(1, upper, 5, on_vector)
        pick_on_vector(1)
        place_on_vector(1)
        hidden(2, lower, 6, on_scalar)
        hidden(2, upper, 7, on_scalar)
        pick_on_scalar(2)
        hidden(3, lower, 0, on_scalar)
        hidden(3, upper, 1, on_scalar)
        wo_codes = keep.tile([P, 4 * E], U8, name="wo_codes", tag="notes0", align_bytes=64)
        nc.sync.dma_start(out=wo_codes[:].bitcast(I32), in_=wo_words[0].rearrange("p e r -> p (e r)").bitcast(I32))
        kf_t = keep.tile([P, PACK], F32, name="kf_t", tag="notes1", align_bytes=64)
        nc.sync.dma_start(out=kf_t[:], in_=kf.rearrange("(p t) o -> p (t o)", t=PACK))
        pick_on_vector(3)
        place_on_scalar(2)

        combine(1)
        combine(0)
        differ(1, 0, I, v[1][:])
        place_on_scalar(LAST)
        differ(0, 0, I, v[0][:])
        combine(2)
        differ(2, 0, I, v[2][:])
        combine(LAST)

        halves = [slice(HALF * h, HALF * (h + 1)) for h in range(2)]
        v_last = [keep.tile([P, HALF], F32, name=f"v_last{h}") for h in range(2)]
        for h in range(2):
            differ(LAST, halves[h].start, halves[h].stop, v_last[h][:])
        w_planes = keep.tile([P, 2, PACK, HALF], BF16, name="w_planes", tag="h1_2", align_bytes=64)
        for t in range(LAST):
            nc.scalar.activation(
                out=w_planes[:, :, t, :], in_=v[t][:].rearrange("p (h i) -> p h i", h=2), func=COPY, scale=kf_t[:, t : t + 1]
            )
        nc.scalar.activation(out=w_planes[:, 0, LAST, :], in_=v_last[0][:], func=COPY, scale=kf_t[:, LAST : LAST + 1])
        nc.vector.tensor_scalar(out=w_planes[:, 1, LAST, :], in0=v_last[1][:], scalar1=kf_t[:, LAST : LAST + 1], scalar2=None, op0=MULT)

        w_woven = [keep.tile([P, HALF, PACK], BF16, name=f"w_woven{h}", align_bytes=64) for h in range(2)]
        for h, copy in ((0, on_scalar), (1, on_vector)):
            copy(
                out=w_woven[h][:].rearrange("p (c i) t -> p c t i", i=4),
                in_=w_planes[:, h, :, :].rearrange("p t (c i) -> p c t i", i=4),
            )
        for h in range(2):
            nc.vector.quantize_mx(
                out=w_codes[:, 4 * HALF * h : 4 * HALF * (h + 1)].bitcast(FP8X4),
                scales=w_sc[:, halves[h]],
                in_=w_woven[h][:].rearrange("p i t -> p (i t)"),
            )

        for h in range(2):
            for m in range(E // P):
                acc = psum.tile([P, HALF], F32, name=f"out_acc{h}{m}", tag=f"bank{2 + 2 * h + m}")
                nc.tensor.matmul_mx(
                    out=acc[:],
                    lhsT=wo_codes[:, 4 * P * m : 4 * P * (m + 1)].bitcast(FP8X4),
                    lhsT_scale=wo_sc[:, P * m : P * (m + 1)],
                    rhs=w_codes[:, 4 * HALF * h : 4 * HALF * (h + 1)].bitcast(FP8X4),
                    rhs_scale=w_sc[:, halves[h]],
                    start=True,
                    stop=True,
                )
                result = keep.tile([P, HALF], F32, name=f"result{h}{m}")
                (on_scalar, on_vector)[m](out=result[:], in_=acc[:])
                nc.sync.dma_start(out=out[P * m : P * (m + 1), halves[h]], in_=result[:])
